import numpy as np
import ml_dtypes


def mxq(x, axis, fmt="e4m3"):
    dtype, down = {"e4m3": (ml_dtypes.float8_e4m3fn, 7), "e5m2": (ml_dtypes.float8_e5m2, 14)}[fmt]
    v = np.moveaxis(np.asarray(x, np.float32).astype(ml_dtypes.bfloat16).astype(np.float64), axis, -1)
    blocks = v.reshape(v.shape[:-1] + (-1, 32))
    amax = np.abs(blocks).max(-1, keepdims=True)
    byte = np.maximum(np.where(amax > 0, np.frexp(amax)[1] - 1 + 127, 0) - down, 1)
    scale = np.exp2(byte - 127.0)
    codes = (blocks / scale).astype(np.float32).astype(dtype).astype(np.float64)
    return np.moveaxis((codes * scale).reshape(v.shape), -1, axis)


WIDE = False


def mx_kscale(k):
    if not WIDE:
        return np.ones(k)
    levels = np.array([10, -10, 5, -5, 0])
    if k % 512:
        return np.exp2(np.random.permutation(np.resize(levels, k // 32))).repeat(32)
    a = np.empty((k // 512, 16))
    for p in range(k // 512):
        a[p, :8] = np.random.permutation(np.resize(levels, 8))
        for g in range(8):
            far = levels[np.abs(levels - a[p, g]) >= 10]
            a[p, g + 8] = far[np.random.randint(len(far))]
    return np.exp2(a.ravel()).repeat(32)


def f64(x):
    return np.asarray(x).astype(np.float64)


def striped(idx):
    return np.tile(idx.reshape(-1, 16).T, (8, 1)).astype(np.uint16)


def unstriped(offs):
    return offs[:16].T.reshape(-1).astype(np.int64)


def pack_weight(w):
    k, n = w.shape
    w = f64(np.asarray(w, np.float32).astype(ml_dtypes.bfloat16)).reshape(k // 32, 32, n)
    amax = np.abs(w).max(1)
    byte = np.clip(np.where(amax > 0, np.frexp(amax)[1] - 1 + 127 - 7, 1), 1, 254)
    scaled = (w * np.exp2(127.0 - byte)[:, None, :]).reshape(k, n).astype(np.float32)
    words = np.ascontiguousarray(scaled.reshape(k // 512, 128, 4, n).transpose(0, 1, 3, 2)).astype(ml_dtypes.float8_e4m3fn).view(np.uint8)
    return words, np.ascontiguousarray(byte.astype(np.uint8).reshape(k // 512, 16, n))


def unpack_weight(words, scales):
    g, p, n, _ = words.shape
    vals = np.ascontiguousarray(words).view(ml_dtypes.float8_e4m3fn).astype(np.float64) * np.repeat(np.exp2(scales.astype(np.float64) - 127.0), 8, axis=1)[..., None]
    return vals.transpose(0, 1, 3, 2).reshape(g * 512, n)


def sigmoid(v):
    return 1.0 / (1.0 + np.exp(-np.maximum(v, -700.0)))


K, T, N, U = 1024, 1024, 128, 2048


def setup_inputs():
    n = np.random.standard_normal
    s = mx_kscale(K)[:, None]
    packed_xT = pack_weight(n((K, T)) * s)
    return {
        "x_words": packed_xT[0],
        "x_scales": packed_xT[1],
        "mem": n((N, U)).astype(np.float32),
        "w1": (n((K, N)) / np.sqrt(K) / s).astype(np.float32),
        "w2": (n((K, N)) / np.sqrt(K) / s).astype(np.float32),
        "slot": striped(np.random.permutation(U)[:T]),
    }


def reference(x_words, x_scales, mem, w1, w2, slot):
    old = f64(mem)[:, unstriped(slot)]
    xq = unpack_weight(x_words, x_scales)
    g = sigmoid(mxq(f64(w2), 0, "e4m3").T @ xq)
    y = np.tanh(mxq(f64(w1), 0, "e4m3").T @ xq)
    out = f64(mem).copy()
    out[:, unstriped(slot)] = old + g * (y - old)
    return out

@@ -1,0 +1,106 @@
+from contextlib import ExitStack
+
+import concourse.mybir as mybir
+
+K, T, N, U = 1024, 1024, 128, 2048
+FLOPS = 2 * 2 * K * T * N
+
+F32 = mybir.dt.float32
+BF16 = mybir.dt.bfloat16
+I32 = mybir.dt.int32
+U32 = mybir.dt.uint32
+U16 = mybir.dt.uint16
+U8 = mybir.dt.uint8
+FP8X4 = mybir.dt.float8_e4m3fn_x4
+ACT = mybir.ActivationFunctionType
+ALU = mybir.AluOpType
+
+P = 128
+PACK = 4
+PASSES = K // (P * PACK)
+CHUNKS = [(0, 256), (256, 256), (512, 512)]
+
+
+def tile_picked_wgmem_tanh_l_kernel(tc, x_words, x_scales, mem, w1, w2, slot, out):
+    nc = tc.nc
+    with ExitStack() as ctx:
+        keep = ctx.enter_context(tc.tile_pool(name="keep", bufs=1))
+        psum = ctx.enter_context(tc.psum_pool(name="psum", bufs=1))
+
+        offsets = keep.tile([P, T // 16], U16, name="offsets")
+        window = keep.tile([P, U], F32, name="window", align_bytes=64)
+        x_plane = keep.tile([P, T], U8, name="x_plane", align_bytes=64)
+        nc.vector.memset(x_plane[:].bitcast(I32), 0)
+        for q in range(4):
+            nc.scalar.dma_start(
+                out=x_plane[32 * q : 32 * q + 8, :].bitcast(I32),
+                in_=x_scales[:, 4 * q : 4 * q + 4, :].bitcast(I32),
+            )
+
+        raw = {}
+        for name, w in (("gate", w2), ("cand", w1)):
+            raw[name] = keep.tile([P, PASSES, PACK, N], F32, name="raw_" + name, align_bytes=64)
+            nc.sync.dma_start(out=raw[name][:], in_=w.rearrange("(z p j) m -> p z j m", z=PASSES, j=PACK))
+
+        words = x_words.rearrange("z p c r -> p z (c r)").bitcast(I32)
+        x_codes = []
+        for c, (c0, width) in enumerate(CHUNKS):
+            x_codes.append(keep.tile([P, PASSES, width], U32, name="x_codes%d" % c, align_bytes=64))
+            nc.sync.dma_start(out=x_codes[c][:].bitcast(I32), in_=words[:, :, c0 : c0 + width])
+            if c == 0:
+                nc.sync.dma_start(offsets[:], slot)
+                nc.sync.dma_start(out=window[:], in_=mem)
+
+        w_codes, w_plane = {}, {}
+        for name in ("gate", "cand"):
+            grouped = keep.tile([P, PASSES, N * PACK], BF16, name="grouped_" + name, align_bytes=64)
+            nc.vector.tensor_copy(
+                out=grouped[:].rearrange("p z (c i j) -> p z c j i", i=4, j=PACK),
+                in_=raw[name][:].rearrange("p z j (c i) -> p z c j i", i=4),
+            )
+            w_codes[name] = keep.tile([P, PASSES * N], U32, name="codes_" + name, align_bytes=64)
+            w_plane[name] = keep.tile([P, PASSES * N], U8, name="plane_" + name, align_bytes=64)
+            nc.vector.quantize_mx(
+                out=w_codes[name][:].bitcast(FP8X4),
+                scales=w_plane[name][:],
+                in_=grouped[:].rearrange("p z w -> p (z w)"),
+            )
+
+        kept = keep.tile([P, T], F32, name="kept", align_bytes=64)
+        fresh = keep.tile([P, T], F32, name="fresh", align_bytes=64)
+
+        def scatter(c0, width):
+            cols = slice(c0, c0 + width)
+            nc.vector.tensor_tensor(
+                window[:].indirect(offsets[:, c0 // 16 : (c0 + width) // 16]), kept[:, cols], fresh[:, cols], ALU.add
+            )
+
+        for c, (c0, width) in enumerate(CHUNKS):
+            cols = slice(c0, c0 + width)
+            acc = {}
+            for name in ("gate", "cand"):
+                acc[name] = psum.tile([P, width], F32, name="acc_%s%d" % (name, c))
+                for z in range(PASSES):
+                    nc.tensor.matmul_mx(
+                        out=acc[name][:],
+                        lhsT=w_codes[name][:, z * N : (z + 1) * N].bitcast(FP8X4),
+                        lhsT_scale=w_plane[name][:, z * N : (z + 1) * N],
+                        rhs=x_codes[c][:, z, :].bitcast(FP8X4),
+                        rhs_scale=x_plane[4 * z : P, cols],
+                        start=(z == 0),
+                        stop=(z == PASSES - 1),
+                    )
+            stay = keep.tile([P, width], F32, name="stay%d" % c, align_bytes=64)
+            gate = keep.tile([P, width], F32, name="gate%d" % c, align_bytes=64)
+            cand = keep.tile([P, width], F32, name="cand%d" % c, align_bytes=64)
+            nc.scalar.activation(stay[:], acc["gate"][:], ACT.Sigmoid, scale=-1.0)
+            nc.scalar.activation(gate[:], acc["gate"][:], ACT.Sigmoid)
+            nc.scalar.activation(cand[:], acc["cand"][:], ACT.Tanh)
+            nc.vector.tensor_tensor(fresh[:, cols], gate[:], cand[:], ALU.mult)
+            nc.vector.tensor_tensor(
+                kept[:, cols], window[:].indirect(offsets[:, c0 // 16 : (c0 + width) // 16]), stay[:], ALU.mult
+            )
+            if c == 0:
+                scatter(c0, width)
+        scatter(CHUNKS[1][0], T - CHUNKS[1][0])
+        nc.sync.dma_start(out=out, in_=window[:])

@@ -18,7 +18,7 @@ ALU = mybir.AluOpType
 P = 128
 PACK = 4
 PASSES = K // (P * PACK)
-CHUNKS = [(0, 256), (256, 256), (512, 512)]
+PIECES = [(0, 256), (256, 256), (512, 512)]
 
 
 def tile_picked_wgmem_tanh_l_kernel(tc, x_words, x_scales, mem, w1, w2, slot, out):
@@ -30,77 +30,108 @@ def tile_picked_wgmem_tanh_l_kernel(tc, x_words, x_scales, mem, w1, w2, slot, ou
         offsets = keep.tile([P, T // 16], U16, name="offsets")
         window = keep.tile([P, U], F32, name="window", align_bytes=64)
         x_plane = keep.tile([P, T], U8, name="x_plane", align_bytes=64)
-        nc.vector.memset(x_plane[:].bitcast(I32), 0)
-        for q in range(4):
-            nc.scalar.dma_start(
-                out=x_plane[32 * q : 32 * q + 8, :].bitcast(I32),
-                in_=x_scales[:, 4 * q : 4 * q + 4, :].bitcast(I32),
-            )
 
-        raw = {}
-        for name, w in (("gate", w2), ("cand", w1)):
-            raw[name] = keep.tile([P, PASSES, PACK, N], F32, name="raw_" + name, align_bytes=64)
-            nc.sync.dma_start(out=raw[name][:], in_=w.rearrange("(z p j) m -> p z j m", z=PASSES, j=PACK))
+        warm = keep.tile([P, 1], F32, name="warm")
+        nc.gpsimd.memset(warm[:], 0.0)
+        nc.scalar.activation(warm[:], warm[:], ACT.Sigmoid)
+
+        def load_weight(name, w):
+            raw = keep.tile([P, PASSES, PACK, N], F32, name="raw_" + name, align_bytes=64)
+            nc.sync.dma_start(out=raw[:], in_=w.rearrange("(z p j) m -> p z j m", z=PASSES, j=PACK))
+            return raw
+
+        def load_scales(queue, cols):
+            for q in range(4):
+                queue.dma_start(
+                    out=x_plane[32 * q : 32 * q + 8, cols].bitcast(I32),
+                    in_=x_scales[:, 4 * q : 4 * q + 4, cols].bitcast(I32),
+                )
 
         words = x_words.rearrange("z p c r -> p z (c r)").bitcast(I32)
-        x_codes = []
-        for c, (c0, width) in enumerate(CHUNKS):
-            x_codes.append(keep.tile([P, PASSES, width], U32, name="x_codes%d" % c, align_bytes=64))
-            nc.sync.dma_start(out=x_codes[c][:].bitcast(I32), in_=words[:, :, c0 : c0 + width])
-            if c == 0:
-                nc.sync.dma_start(offsets[:], slot)
-                nc.sync.dma_start(out=window[:], in_=mem)
+
+        def load_codes(c):
+            c0, width = PIECES[c]
+            codes = keep.tile([P, PASSES, width], U32, name="x_codes%d" % c, align_bytes=64)
+            nc.sync.dma_start(out=codes[:].bitcast(I32), in_=words[:, :, c0 : c0 + width])
+            return codes
+
+        load_scales(nc.scalar, slice(0, T // 2))
+        raw_cand = load_weight("cand", w1)
+        raw_gate = load_weight("gate", w2)
+        x_codes = [load_codes(0)]
+        nc.sync.dma_start(offsets[:], slot)
+        nc.sync.dma_start(out=window[:], in_=mem)
+        x_codes.append(load_codes(1))
+        load_scales(nc.sync, slice(T // 2, T))
+        x_codes.append(load_codes(2))
 
         w_codes, w_plane = {}, {}
-        for name in ("gate", "cand"):
-            grouped = keep.tile([P, PASSES, N * PACK], BF16, name="grouped_" + name, align_bytes=64)
-            nc.vector.tensor_copy(
-                out=grouped[:].rearrange("p z (c i j) -> p z c j i", i=4, j=PACK),
-                in_=raw[name][:].rearrange("p z j (c i) -> p z c j i", i=4),
-            )
+        for name in ("cand", "gate"):
             w_codes[name] = keep.tile([P, PASSES * N], U32, name="codes_" + name, align_bytes=64)
             w_plane[name] = keep.tile([P, PASSES * N], U8, name="plane_" + name, align_bytes=64)
+
+        def quantise(copy, run, name, raw, z0, passes):
+            grouped = keep.tile([P, passes, N * PACK], BF16, name="grouped_%s%d" % (name, z0), align_bytes=64)
+            copy(
+                out=grouped[:].rearrange("p z (c i j) -> p z c j i", i=run, j=PACK),
+                in_=raw[:, z0 : z0 + passes].rearrange("p z j (c i) -> p z c j i", i=run),
+            )
+            cols = slice(z0 * N, (z0 + passes) * N)
             nc.vector.quantize_mx(
-                out=w_codes[name][:].bitcast(FP8X4),
-                scales=w_plane[name][:],
+                out=w_codes[name][:, cols].bitcast(FP8X4),
+                scales=w_plane[name][:, cols],
                 in_=grouped[:].rearrange("p z w -> p (z w)"),
             )
+
+        quantise(nc.vector.tensor_copy, 4, "cand", raw_cand, 0, PASSES)
+        quantise(nc.scalar.copy, 1, "gate", raw_gate, 0, 1)
+        quantise(nc.vector.tensor_copy, 4, "gate", raw_gate, 1, 1)
 
         kept = keep.tile([P, T], F32, name="kept", align_bytes=64)
         fresh = keep.tile([P, T], F32, name="fresh", align_bytes=64)
 
+        def by_slot(c0, width):
+            return window[:].indirect(offsets[:, c0 // 16 : (c0 + width) // 16])
+
         def scatter(c0, width):
             cols = slice(c0, c0 + width)
-            nc.vector.tensor_tensor(
-                window[:].indirect(offsets[:, c0 // 16 : (c0 + width) // 16]), kept[:, cols], fresh[:, cols], ALU.add
-            )
+            nc.vector.tensor_tensor(by_slot(c0, width), kept[:, cols], fresh[:, cols], ALU.add)
 
-        for c, (c0, width) in enumerate(CHUNKS):
+        def product(name, c):
+            c0, width = PIECES[c]
+            acc = psum.tile([P, width], F32, name="acc_%s%d" % (name, c))
+            for z in range(PASSES):
+                nc.tensor.matmul_mx(
+                    out=acc[:],
+                    lhsT=w_codes[name][:, z * N : (z + 1) * N].bitcast(FP8X4),
+                    lhsT_scale=w_plane[name][:, z * N : (z + 1) * N],
+                    rhs=x_codes[c][:, z, :].bitcast(FP8X4),
+                    rhs_scale=x_plane[4 * z : P, c0 : c0 + width],
+                    start=(z == 0),
+                    stop=(z == PASSES - 1),
+                )
+            return acc
+
+        for c, (c0, width) in enumerate(PIECES):
             cols = slice(c0, c0 + width)
-            acc = {}
-            for name in ("gate", "cand"):
-                acc[name] = psum.tile([P, width], F32, name="acc_%s%d" % (name, c))
-                for z in range(PASSES):
-                    nc.tensor.matmul_mx(
-                        out=acc[name][:],
-                        lhsT=w_codes[name][:, z * N : (z + 1) * N].bitcast(FP8X4),
-                        lhsT_scale=w_plane[name][:, z * N : (z + 1) * N],
-                        rhs=x_codes[c][:, z, :].bitcast(FP8X4),
-                        rhs_scale=x_plane[4 * z : P, cols],
-                        start=(z == 0),
-                        stop=(z == PASSES - 1),
-                    )
             stay = keep.tile([P, width], F32, name="stay%d" % c, align_bytes=64)
             gate = keep.tile([P, width], F32, name="gate%d" % c, align_bytes=64)
             cand = keep.tile([P, width], F32, name="cand%d" % c, align_bytes=64)
-            nc.scalar.activation(stay[:], acc["gate"][:], ACT.Sigmoid, scale=-1.0)
-            nc.scalar.activation(gate[:], acc["gate"][:], ACT.Sigmoid)
-            nc.scalar.activation(cand[:], acc["cand"][:], ACT.Tanh)
-            nc.vector.tensor_tensor(fresh[:, cols], gate[:], cand[:], ALU.mult)
-            nc.vector.tensor_tensor(
-                kept[:, cols], window[:].indirect(offsets[:, c0 // 16 : (c0 + width) // 16]), stay[:], ALU.mult
-            )
             if c == 0:
+                nc.scalar.activation(cand[:], product("cand", c)[:], ACT.Tanh)
+                logit = product("gate", c)
+                nc.scalar.activation(gate[:], logit[:], ACT.Sigmoid)
+                nc.scalar.activation(stay[:], logit[:], ACT.Sigmoid, scale=-1.0)
+                nc.vector.tensor_tensor(fresh[:, cols], gate[:], cand[:], ALU.mult)
+                nc.vector.tensor_tensor(kept[:, cols], by_slot(c0, width), stay[:], ALU.mult)
                 scatter(c0, width)
-        scatter(CHUNKS[1][0], T - CHUNKS[1][0])
-        nc.sync.dma_start(out=out, in_=window[:])
+            else:
+                logit = product("gate", c)
+                nc.scalar.activation(stay[:], logit[:], ACT.Sigmoid, scale=-1.0)
+                nc.scalar.activation(gate[:], logit[:], ACT.Sigmoid)
+                nc.scalar.activation(cand[:], product("cand", c)[:], ACT.Tanh)
+                nc.vector.tensor_tensor(fresh[:, cols], gate[:], cand[:], ALU.mult)
+                nc.vector.tensor_tensor(kept[:, cols], by_slot(c0, width), stay[:], ALU.mult)
+        scatter(PIECES[1][0], T - PIECES[1][0])
+        nc.sync.dma_start(out=out[:, : U // 2], in_=window[:, : U // 2])
+        nc.scalar.dma_start(out=out[:, U // 2 :], in_=window[:, U // 2 :])

@@ -18,7 +18,7 @@ ALU = mybir.AluOpType
 P = 128
 PACK = 4
 PASSES = K // (P * PACK)
-PIECES = [(0, 256), (256, 256), (512, 512)]
+LOADS = [(0, 256), (256, 256), (512, 512)]
 
 
 def tile_picked_wgmem_tanh_l_kernel(tc, x_words, x_scales, mem, w1, w2, slot, out):
@@ -35,13 +35,8 @@ def tile_picked_wgmem_tanh_l_kernel(tc, x_words, x_scales, mem, w1, w2, slot, ou
         nc.gpsimd.memset(warm[:], 0.0)
         nc.scalar.activation(warm[:], warm[:], ACT.Sigmoid)
 
-        def load_weight(name, w):
-            raw = keep.tile([P, PASSES, PACK, N], F32, name="raw_" + name, align_bytes=64)
-            nc.sync.dma_start(out=raw[:], in_=w.rearrange("(z p j) m -> p z j m", z=PASSES, j=PACK))
-            return raw
-
-        def load_scales(queue, cols):
-            for q in range(4):
+        def load_scales(queue, cols, quadrants):
+            for q in quadrants:
                 queue.dma_start(
                     out=x_plane[32 * q : 32 * q + 8, cols].bitcast(I32),
                     in_=x_scales[:, 4 * q : 4 * q + 4, cols].bitcast(I32),
@@ -50,88 +45,122 @@ def tile_picked_wgmem_tanh_l_kernel(tc, x_words, x_scales, mem, w1, w2, slot, ou
         words = x_words.rearrange("z p c r -> p z (c r)").bitcast(I32)
 
         def load_codes(c):
-            c0, width = PIECES[c]
+            c0, width = LOADS[c]
             codes = keep.tile([P, PASSES, width], U32, name="x_codes%d" % c, align_bytes=64)
             nc.sync.dma_start(out=codes[:].bitcast(I32), in_=words[:, :, c0 : c0 + width])
             return codes
 
-        load_scales(nc.scalar, slice(0, T // 2))
-        raw_cand = load_weight("cand", w1)
-        raw_gate = load_weight("gate", w2)
+        load_scales(nc.scalar, slice(0, T // 2), range(2))
+        raw = {}
+
+        def load_weight(name, w):
+            both = keep.tile([P, PASSES, PACK, N], F32, name="raw_" + name, align_bytes=64)
+            nc.sync.dma_start(out=both[:], in_=w.rearrange("(z p j) m -> p z j m", z=PASSES, j=PACK))
+            for z in range(PASSES):
+                raw[name, z] = both[:, z]
+
+        load_weight("cand", w1)
+        load_scales(nc.sync, slice(0, T // 2), range(2, 4))
+        load_weight("gate", w2)
         x_codes = [load_codes(0)]
         nc.sync.dma_start(offsets[:], slot)
         nc.sync.dma_start(out=window[:], in_=mem)
         x_codes.append(load_codes(1))
-        load_scales(nc.sync, slice(T // 2, T))
+        load_scales(nc.sync, slice(T // 2, T), range(4))
         x_codes.append(load_codes(2))
-
-        w_codes, w_plane = {}, {}
-        for name in ("cand", "gate"):
-            w_codes[name] = keep.tile([P, PASSES * N], U32, name="codes_" + name, align_bytes=64)
-            w_plane[name] = keep.tile([P, PASSES * N], U8, name="plane_" + name, align_bytes=64)
-
-        def quantise(copy, run, name, raw, z0, passes):
-            grouped = keep.tile([P, passes, N * PACK], BF16, name="grouped_%s%d" % (name, z0), align_bytes=64)
-            copy(
-                out=grouped[:].rearrange("p z (c i j) -> p z c j i", i=run, j=PACK),
-                in_=raw[:, z0 : z0 + passes].rearrange("p z j (c i) -> p z c j i", i=run),
-            )
-            cols = slice(z0 * N, (z0 + passes) * N)
-            nc.vector.quantize_mx(
-                out=w_codes[name][:, cols].bitcast(FP8X4),
-                scales=w_plane[name][:, cols],
-                in_=grouped[:].rearrange("p z w -> p (z w)"),
-            )
-
-        quantise(nc.vector.tensor_copy, 4, "cand", raw_cand, 0, PASSES)
-        quantise(nc.scalar.copy, 1, "gate", raw_gate, 0, 1)
-        quantise(nc.vector.tensor_copy, 4, "gate", raw_gate, 1, 1)
-
-        kept = keep.tile([P, T], F32, name="kept", align_bytes=64)
-        fresh = keep.tile([P, T], F32, name="fresh", align_bytes=64)
 
         def by_slot(c0, width):
             return window[:].indirect(offsets[:, c0 // 16 : (c0 + width) // 16])
 
-        def scatter(c0, width):
-            cols = slice(c0, c0 + width)
-            nc.vector.tensor_tensor(by_slot(c0, width), kept[:, cols], fresh[:, cols], ALU.add)
+        def x_operands(z, c0, width):
+            c = [i for i, (l0, lw) in enumerate(LOADS) if l0 <= c0 < l0 + lw][0]
+            l0 = LOADS[c][0]
+            return x_codes[c][:, z, c0 - l0 : c0 - l0 + width].bitcast(FP8X4), x_plane[4 * z : P, c0 : c0 + width]
 
-        def product(name, c):
-            c0, width = PIECES[c]
-            acc = psum.tile([P, width], F32, name="acc_%s%d" % (name, c))
+        w_codes, w_plane, grouped = {}, {}, {}
+
+        def regroup(copy, name, z, m0, m1):
+            copy(
+                out=grouped[name, z][:, m0 * PACK : m1 * PACK].rearrange("p (c i j) -> p c j i", i=4, j=PACK),
+                in_=raw[name, z][:, :, m0:m1].rearrange("p j (c i) -> p c j i", i=4),
+            )
+
+        def quantise(name, z):
+            w_codes[name, z] = keep.tile([P, N], U32, name="codes_%s%d" % (name, z), align_bytes=64)
+            w_plane[name, z] = keep.tile([P, N], U8, name="plane_%s%d" % (name, z), align_bytes=64)
+            nc.vector.quantize_mx(out=w_codes[name, z][:].bitcast(FP8X4), scales=w_plane[name, z][:], in_=grouped[name, z][:])
+
+        for name in ("gate", "cand"):
             for z in range(PASSES):
+                grouped[name, z] = keep.tile([P, N * PACK], BF16, name="grouped_%s%d" % (name, z), align_bytes=64)
+
+        def product(name, c0, width, bank):
+            acc = psum.tile([P, width], F32, name="acc_%s%d" % (name, c0), tag=bank)
+            for z in range(PASSES):
+                codes, plane = x_operands(z, c0, width)
                 nc.tensor.matmul_mx(
                     out=acc[:],
-                    lhsT=w_codes[name][:, z * N : (z + 1) * N].bitcast(FP8X4),
-                    lhsT_scale=w_plane[name][:, z * N : (z + 1) * N],
-                    rhs=x_codes[c][:, z, :].bitcast(FP8X4),
-                    rhs_scale=x_plane[4 * z : P, c0 : c0 + width],
+                    lhsT=w_codes[name, z][:].bitcast(FP8X4),
+                    lhsT_scale=w_plane[name, z][:],
+                    rhs=codes,
+                    rhs_scale=plane,
                     start=(z == 0),
                     stop=(z == PASSES - 1),
                 )
             return acc
 
-        for c, (c0, width) in enumerate(PIECES):
+        regroup(nc.vector.tensor_copy, "cand", 0, 0, N)
+        regroup(nc.scalar.copy, "cand", 1, 0, N)
+        quantise("cand", 0)
+        quantise("cand", 1)
+        regroup(nc.vector.tensor_copy, "gate", 0, 0, N)
+        regroup(nc.scalar.copy, "gate", 1, N // 2, N)
+        regroup(nc.vector.tensor_copy, "gate", 1, 0, N // 2)
+        quantise("gate", 0)
+        quantise("gate", 1)
+
+        stay = keep.tile([P, T], F32, name="stay", align_bytes=64)
+        minus_cand = keep.tile([P, T], F32, name="minus_cand", align_bytes=64)
+        kept = keep.tile([P, T], F32, name="kept", align_bytes=64)
+        fresh = keep.tile([P, T], F32, name="fresh", align_bytes=64)
+
+        def candidates(c0, width):
+            acc = product("cand", c0, width, "cand%d" % c0)
+            nc.scalar.activation(minus_cand[:, c0 : c0 + width], acc[:], ACT.Tanh, scale=-1.0)
+
+        def gates(c0, width):
+            acc = product("gate", c0, width, "gate%d" % c0)
+            nc.scalar.activation(stay[:, c0 : c0 + width], acc[:], ACT.Sigmoid, scale=-1.0)
+
+        def blend(c0, width):
             cols = slice(c0, c0 + width)
-            stay = keep.tile([P, width], F32, name="stay%d" % c, align_bytes=64)
-            gate = keep.tile([P, width], F32, name="gate%d" % c, align_bytes=64)
-            cand = keep.tile([P, width], F32, name="cand%d" % c, align_bytes=64)
-            if c == 0:
-                nc.scalar.activation(cand[:], product("cand", c)[:], ACT.Tanh)
-                logit = product("gate", c)
-                nc.scalar.activation(gate[:], logit[:], ACT.Sigmoid)
-                nc.scalar.activation(stay[:], logit[:], ACT.Sigmoid, scale=-1.0)
-                nc.vector.tensor_tensor(fresh[:, cols], gate[:], cand[:], ALU.mult)
-                nc.vector.tensor_tensor(kept[:, cols], by_slot(c0, width), stay[:], ALU.mult)
-                scatter(c0, width)
-            else:
-                logit = product("gate", c)
-                nc.scalar.activation(stay[:], logit[:], ACT.Sigmoid, scale=-1.0)
-                nc.scalar.activation(gate[:], logit[:], ACT.Sigmoid)
-                nc.scalar.activation(cand[:], product("cand", c)[:], ACT.Tanh)
-                nc.vector.tensor_tensor(fresh[:, cols], gate[:], cand[:], ALU.mult)
-                nc.vector.tensor_tensor(kept[:, cols], by_slot(c0, width), stay[:], ALU.mult)
-        scatter(PIECES[1][0], T - PIECES[1][0])
+            nc.vector.scalar_tensor_tensor(fresh[:, cols], stay[:, cols], 1.0, minus_cand[:, cols], ALU.subtract, ALU.mult)
+
+        def gather(c0, width):
+            cols = slice(c0, c0 + width)
+            nc.vector.tensor_tensor(kept[:, cols], by_slot(c0, width), stay[:, cols], ALU.mult)
+
+        def scatter(c0, width):
+            cols = slice(c0, c0 + width)
+            nc.vector.tensor_tensor(by_slot(c0, width), kept[:, cols], fresh[:, cols], ALU.add)
+
+        candidates(0, 256)
+        gates(0, 256)
+        blend(0, 256)
+        gather(0, 256)
+        scatter(0, 256)
+        gates(256, 256)
+        candidates(256, 256)
+        gates(512, 256)
+        gates(768, 256)
+        candidates(512, 256)
+        candidates(768, 256)
+        blend(256, 256)
+        gather(256, 256)
+        gather(512, 256)
+        gather(768, 256)
+        blend(512, 512)
+        scatter(256, 768)
+
         nc.sync.dma_start(out=out[:, : U // 2], in_=window[:, : U // 2])
         nc.scalar.dma_start(out=out[:, U // 2 :], in_=window[:, U // 2 :])

@@ -63,8 +63,8 @@ def tile_picked_wgmem_tanh_l_kernel(tc, x_words, x_scales, mem, w1, w2, slot, ou
         load_scales(nc.sync, slice(0, T // 2), range(2, 4))
         load_weight("gate", w2)
         x_codes = [load_codes(0)]
-        nc.sync.dma_start(offsets[:], slot)
         nc.sync.dma_start(out=window[:], in_=mem)
+        nc.sync.dma_start(offsets[:], slot)
         x_codes.append(load_codes(1))
         load_scales(nc.sync, slice(T // 2, T), range(4))
         x_codes.append(load_codes(2))
@@ -151,16 +151,13 @@ def tile_picked_wgmem_tanh_l_kernel(tc, x_words, x_scales, mem, w1, w2, slot, ou
         scatter(0, 256)
         gates(256, 256)
         candidates(256, 256)
-        gates(512, 256)
-        gates(768, 256)
-        candidates(512, 256)
-        candidates(768, 256)
         blend(256, 256)
         gather(256, 256)
-        gather(512, 256)
-        gather(768, 256)
-        blend(512, 512)
+        for c0 in (512, 768):
+            gates(c0, 256)
+            candidates(c0, 256)
+            gather(c0, 256)
+            blend(c0, 256)
         scatter(256, 768)
 
-        nc.sync.dma_start(out=out[:, : U // 2], in_=window[:, : U // 2])
-        nc.scalar.dma_start(out=out[:, U // 2 :], in_=window[:, U // 2 :])
+        nc.sync.dma_start(out=out, in_=window[:])

@@ -125,7 +125,7 @@ def tile_picked_wgmem_tanh_l_kernel(tc, x_words, x_scales, mem, w1, w2, slot, ou
         fresh = keep.tile([P, T], F32, name="fresh", align_bytes=64)
 
         def candidates(c0, width):
-            acc = product("cand", c0, width, "cand%d" % c0)
+            acc = product("cand", c0, width, "cand%d" % (c0 % 768))
             nc.scalar.activation(minus_cand[:, c0 : c0 + width], acc[:], ACT.Tanh, scale=-1.0)
 
         def gates(c0, width):
@@ -145,8 +145,9 @@ def tile_picked_wgmem_tanh_l_kernel(tc, x_words, x_scales, mem, w1, w2, slot, ou
             nc.vector.tensor_tensor(by_slot(c0, width), kept[:, cols], fresh[:, cols], ALU.add)
 
         candidates(0, 256)
-        gates(0, 256)
-        blend(0, 256)
+        for c0 in (0, 128):
+            gates(c0, 128)
+            blend(c0, 128)
         gather(0, 256)
         scatter(0, 256)
         gates(256, 256)

@@ -31,10 +31,6 @@ def tile_picked_wgmem_tanh_l_kernel(tc, x_words, x_scales, mem, w1, w2, slot, ou
         window = keep.tile([P, U], F32, name="window", align_bytes=64)
         x_plane = keep.tile([P, T], U8, name="x_plane", align_bytes=64)
 
-        warm = keep.tile([P, 1], F32, name="warm")
-        nc.gpsimd.memset(warm[:], 0.0)
-        nc.scalar.activation(warm[:], warm[:], ACT.Sigmoid)
-
         def load_scales(queue, cols, quadrants):
             for q in quadrants:
                 queue.dma_start(
@@ -59,9 +55,9 @@ def tile_picked_wgmem_tanh_l_kernel(tc, x_words, x_scales, mem, w1, w2, slot, ou
             for z in range(PASSES):
                 raw[name, z] = both[:, z]
 
-        load_weight("cand", w1)
-        load_scales(nc.sync, slice(0, T // 2), range(2, 4))
         load_weight("gate", w2)
+        load_scales(nc.sync, slice(0, T // 2), range(2, 4))
+        load_weight("cand", w1)
         x_codes = [load_codes(0)]
         nc.sync.dma_start(out=window[:], in_=mem)
         nc.sync.dma_start(offsets[:], slot)
@@ -109,15 +105,11 @@ def tile_picked_wgmem_tanh_l_kernel(tc, x_words, x_scales, mem, w1, w2, slot, ou
                 )
             return acc
 
-        regroup(nc.vector.tensor_copy, "cand", 0, 0, N)
-        regroup(nc.scalar.copy, "cand", 1, 0, N)
-        quantise("cand", 0)
-        quantise("cand", 1)
-        regroup(nc.vector.tensor_copy, "gate", 0, 0, N)
-        regroup(nc.scalar.copy, "gate", 1, N // 2, N)
-        regroup(nc.vector.tensor_copy, "gate", 1, 0, N // 2)
-        quantise("gate", 0)
-        quantise("gate", 1)
+        for name in ("gate", "cand"):
+            for z in range(PASSES):
+                regroup(nc.vector.tensor_copy, name, z, 0, N)
+            for z in range(PASSES):
+                quantise(name, z)
 
         stay = keep.tile([P, T], F32, name="stay", align_bytes=64)
         minus_cand = keep.tile([P, T], F32, name="minus_cand", align_bytes=64)
@@ -125,11 +117,11 @@ def tile_picked_wgmem_tanh_l_kernel(tc, x_words, x_scales, mem, w1, w2, slot, ou
         fresh = keep.tile([P, T], F32, name="fresh", align_bytes=64)
 
         def candidates(c0, width):
-            acc = product("cand", c0, width, "cand%d" % (c0 % 768))
+            acc = product("cand", c0, width, "cand%d" % c0)
             nc.scalar.activation(minus_cand[:, c0 : c0 + width], acc[:], ACT.Tanh, scale=-1.0)
 
         def gates(c0, width):
-            acc = product("gate", c0, width, "gate%d" % c0)
+            acc = product("gate", c0, width, "gate%d" % (c0 % 768))
             nc.scalar.activation(stay[:, c0 : c0 + width], acc[:], ACT.Sigmoid, scale=-1.0)
 
         def blend(c0, width):
@@ -144,9 +136,9 @@ def tile_picked_wgmem_tanh_l_kernel(tc, x_words, x_scales, mem, w1, w2, slot, ou
             cols = slice(c0, c0 + width)
             nc.vector.tensor_tensor(by_slot(c0, width), kept[:, cols], fresh[:, cols], ALU.add)
 
-        candidates(0, 256)
+        gates(0, 256)
         for c0 in (0, 128):
-            gates(c0, 128)
+            candidates(c0, 128)
             blend(c0, 128)
         gather(0, 256)
         scatter(0, 256)

@@ -29,13 +29,13 @@ def tile_picked_wgmem_tanh_l_kernel(tc, x_words, x_scales, mem, w1, w2, slot, ou
 
         offsets = keep.tile([P, T // 16], U16, name="offsets")
         window = keep.tile([P, U], F32, name="window", align_bytes=64)
-        x_plane = keep.tile([P, T], U8, name="x_plane", align_bytes=64)
+        x_plane = keep.tile([P, PASSES, T], U8, name="x_plane", align_bytes=64)
 
         def load_scales(queue, cols, quadrants):
             for q in quadrants:
                 queue.dma_start(
-                    out=x_plane[32 * q : 32 * q + 8, cols].bitcast(I32),
-                    in_=x_scales[:, 4 * q : 4 * q + 4, cols].bitcast(I32),
+                    out=x_plane[32 * q : 32 * q + 4, :, cols].bitcast(I32),
+                    in_=x_scales[:, 4 * q : 4 * q + 4, cols].rearrange("z r c -> r z c").bitcast(I32),
                 )
 
         words = x_words.rearrange("z p c r -> p z (c r)").bitcast(I32)
@@ -71,7 +71,7 @@ def tile_picked_wgmem_tanh_l_kernel(tc, x_words, x_scales, mem, w1, w2, slot, ou
         def x_operands(z, c0, width):
             c = [i for i, (l0, lw) in enumerate(LOADS) if l0 <= c0 < l0 + lw][0]
             l0 = LOADS[c][0]
-            return x_codes[c][:, z, c0 - l0 : c0 - l0 + width].bitcast(FP8X4), x_plane[4 * z : P, c0 : c0 + width]
+            return x_codes[c][:, z, c0 - l0 : c0 - l0 + width].bitcast(FP8X4), x_plane[:, z, c0 : c0 + width]
 
         w_codes, w_plane, grouped = {}, {}, {}
 
@@ -146,11 +146,12 @@ def tile_picked_wgmem_tanh_l_kernel(tc, x_words, x_scales, mem, w1, w2, slot, ou
         candidates(256, 256)
         blend(256, 256)
         gather(256, 256)
-        for c0 in (512, 768):
-            gates(c0, 256)
-            candidates(c0, 256)
-            gather(c0, 256)
-            blend(c0, 256)
+        gates(512, 256)
+        gates(768, 256)
+        candidates(512, 256)
+        candidates(768, 256)
+        gather(512, 512)
+        blend(512, 512)
         scatter(256, 768)
 
         nc.sync.dma_start(out=out, in_=window[:])

@@ -18,7 +18,7 @@ ALU = mybir.AluOpType
 P = 128
 PACK = 4
 PASSES = K // (P * PACK)
-LOADS = [(0, 256), (256, 256), (512, 512)]
+LOADS = [(0, 512), (512, 256), (768, 256)]
 
 
 def tile_picked_wgmem_tanh_l_kernel(tc, x_words, x_scales, mem, w1, w2, slot, out):
@@ -57,12 +57,12 @@ def tile_picked_wgmem_tanh_l_kernel(tc, x_words, x_scales, mem, w1, w2, slot, ou
 
         load_weight("gate", w2)
         load_scales(nc.sync, slice(0, T // 2), range(2, 4))
-        load_weight("cand", w1)
         x_codes = [load_codes(0)]
+        load_weight("cand", w1)
         nc.sync.dma_start(out=window[:], in_=mem)
         nc.sync.dma_start(offsets[:], slot)
-        x_codes.append(load_codes(1))
         load_scales(nc.sync, slice(T // 2, T), range(4))
+        x_codes.append(load_codes(1))
         x_codes.append(load_codes(2))
 
         def by_slot(c0, width):
@@ -107,22 +107,24 @@ def tile_picked_wgmem_tanh_l_kernel(tc, x_words, x_scales, mem, w1, w2, slot, ou
 
         for name in ("gate", "cand"):
             for z in range(PASSES):
-                regroup(nc.vector.tensor_copy, name, z, 0, N)
+                regroup(nc.scalar.copy if (name, z) == ("cand", 1) else nc.vector.tensor_copy, name, z, 0, N)
             for z in range(PASSES):
                 quantise(name, z)
 
         stay = keep.tile([P, T], F32, name="stay", align_bytes=64)
         minus_cand = keep.tile([P, T], F32, name="minus_cand", align_bytes=64)
+        old = keep.tile([P, 448], F32, name="old", align_bytes=64)
         kept = keep.tile([P, T], F32, name="kept", align_bytes=64)
         fresh = keep.tile([P, T], F32, name="fresh", align_bytes=64)
+        new_b = keep.tile([P, 256], F32, name="new_b", align_bytes=64)
 
-        def candidates(c0, width):
-            acc = product("cand", c0, width, "cand%d" % c0)
-            nc.scalar.activation(minus_cand[:, c0 : c0 + width], acc[:], ACT.Tanh, scale=-1.0)
+        def candidates(c0):
+            acc = product("cand", c0, 256, "cand%d" % c0)
+            nc.scalar.activation(minus_cand[:, c0 : c0 + 256], acc[:], ACT.Tanh, scale=-1.0)
 
-        def gates(c0, width):
-            acc = product("gate", c0, width, "gate%d" % (c0 % 768))
-            nc.scalar.activation(stay[:, c0 : c0 + width], acc[:], ACT.Sigmoid, scale=-1.0)
+        def gates(c0):
+            acc = product("gate", c0, 256, "gate%d" % c0)
+            nc.scalar.activation(stay[:, c0 : c0 + 256], acc[:], ACT.Sigmoid, scale=-1.0)
 
         def blend(c0, width):
             cols = slice(c0, c0 + width)
@@ -136,22 +138,22 @@ def tile_picked_wgmem_tanh_l_kernel(tc, x_words, x_scales, mem, w1, w2, slot, ou
             cols = slice(c0, c0 + width)
             nc.vector.tensor_tensor(by_slot(c0, width), kept[:, cols], fresh[:, cols], ALU.add)
 
-        gates(0, 256)
-        for c0 in (0, 128):
-            candidates(c0, 128)
-            blend(c0, 128)
-        gather(0, 256)
+        gates(0)
+        gates(256)
+        for c0 in (0, 256):
+            candidates(c0)
+            blend(c0, 256)
+        gather(0, 512)
+        nc.vector.tensor_tensor(new_b[:], kept[:, 256:512], fresh[:, 256:512], ALU.add)
+        nc.scalar.activation(old[:], by_slot(512, 448), ACT.Copy)
         scatter(0, 256)
-        gates(256, 256)
-        candidates(256, 256)
-        blend(256, 256)
-        gather(256, 256)
-        gates(512, 256)
-        gates(768, 256)
-        candidates(512, 256)
-        candidates(768, 256)
-        gather(512, 512)
+        for c0 in (512, 768):
+            candidates(c0)
+            gates(c0)
+        gather(960, 64)
+        nc.scalar.activation(by_slot(256, 256), new_b[:], ACT.Copy)
+        nc.vector.tensor_tensor(kept[:, 512:960], old[:], stay[:, 512:960], ALU.mult)
         blend(512, 512)
-        scatter(256, 768)
+        scatter(512, 512)
 
         nc.sync.dma_start(out=out, in_=window[:])

@@ -18,7 +18,7 @@ ALU = mybir.AluOpType
 P = 128
 PACK = 4
 PASSES = K // (P * PACK)
-LOADS = [(0, 512), (512, 256), (768, 256)]
+LOADS = [(0, 256), (256, 256), (512, 256), (768, 256)]
 
 
 def tile_picked_wgmem_tanh_l_kernel(tc, x_words, x_scales, mem, w1, w2, slot, out):
@@ -46,7 +46,8 @@ def tile_picked_wgmem_tanh_l_kernel(tc, x_words, x_scales, mem, w1, w2, slot, ou
             nc.sync.dma_start(out=codes[:].bitcast(I32), in_=words[:, :, c0 : c0 + width])
             return codes
 
-        load_scales(nc.scalar, slice(0, T // 2), range(2))
+        load_scales(nc.scalar, slice(0, T), range(1))
+        load_scales(nc.scalar, slice(0, T // 2), range(1, 2))
         raw = {}
 
         def load_weight(name, w):
@@ -57,13 +58,13 @@ def tile_picked_wgmem_tanh_l_kernel(tc, x_words, x_scales, mem, w1, w2, slot, ou
 
         load_weight("gate", w2)
         load_scales(nc.sync, slice(0, T // 2), range(2, 4))
-        x_codes = [load_codes(0)]
         load_weight("cand", w1)
+        x_codes = [load_codes(0), load_codes(1)]
         nc.sync.dma_start(out=window[:], in_=mem)
         nc.sync.dma_start(offsets[:], slot)
-        load_scales(nc.sync, slice(T // 2, T), range(4))
-        x_codes.append(load_codes(1))
+        load_scales(nc.sync, slice(T // 2, T), range(1, 4))
         x_codes.append(load_codes(2))
+        x_codes.append(load_codes(3))
 
         def by_slot(c0, width):
             return window[:].indirect(offsets[:, c0 // 16 : (c0 + width) // 16])
@@ -107,7 +108,7 @@ def tile_picked_wgmem_tanh_l_kernel(tc, x_words, x_scales, mem, w1, w2, slot, ou
 
         for name in ("gate", "cand"):
             for z in range(PASSES):
-                regroup(nc.scalar.copy if (name, z) == ("cand", 1) else nc.vector.tensor_copy, name, z, 0, N)
+                regroup(nc.vector.tensor_copy, name, z, 0, N)
             for z in range(PASSES):
                 quantise(name, z)
 
@@ -126,9 +127,9 @@ def tile_picked_wgmem_tanh_l_kernel(tc, x_words, x_scales, mem, w1, w2, slot, ou
             acc = product("gate", c0, 256, "gate%d" % c0)
             nc.scalar.activation(stay[:, c0 : c0 + 256], acc[:], ACT.Sigmoid, scale=-1.0)
 
-        def blend(c0, width):
+        def blend(c0, width, dst=fresh):
             cols = slice(c0, c0 + width)
-            nc.vector.scalar_tensor_tensor(fresh[:, cols], stay[:, cols], 1.0, minus_cand[:, cols], ALU.subtract, ALU.mult)
+            nc.vector.scalar_tensor_tensor(dst[:, cols], stay[:, cols], 1.0, minus_cand[:, cols], ALU.subtract, ALU.mult)
 
         def gather(c0, width):
             cols = slice(c0, c0 + width)
@@ -138,15 +139,16 @@ def tile_picked_wgmem_tanh_l_kernel(tc, x_words, x_scales, mem, w1, w2, slot, ou
             cols = slice(c0, c0 + width)
             nc.vector.tensor_tensor(by_slot(c0, width), kept[:, cols], fresh[:, cols], ALU.add)
 
-        gates(0)
-        gates(256)
         for c0 in (0, 256):
+            gates(c0)
             candidates(c0)
-            blend(c0, 256)
-        gather(0, 512)
-        nc.vector.tensor_tensor(new_b[:], kept[:, 256:512], fresh[:, 256:512], ALU.add)
+        blend(0, 256)
+        gather(256, 256)
+        gather(0, 256)
+        blend(256, 256, stay)
         nc.scalar.activation(old[:], by_slot(512, 448), ACT.Copy)
         scatter(0, 256)
+        nc.vector.tensor_tensor(new_b[:], kept[:, 256:512], stay[:, 256:512], ALU.add)
         for c0 in (512, 768):
             candidates(c0)
             gates(c0)

@@ -46,8 +46,7 @@ def tile_picked_wgmem_tanh_l_kernel(tc, x_words, x_scales, mem, w1, w2, slot, ou
             nc.sync.dma_start(out=codes[:].bitcast(I32), in_=words[:, :, c0 : c0 + width])
             return codes
 
-        load_scales(nc.scalar, slice(0, T), range(1))
-        load_scales(nc.scalar, slice(0, T // 2), range(1, 2))
+        load_scales(nc.scalar, slice(0, T), range(2))
         raw = {}
 
         def load_weight(name, w):
@@ -62,9 +61,11 @@ def tile_picked_wgmem_tanh_l_kernel(tc, x_words, x_scales, mem, w1, w2, slot, ou
         x_codes = [load_codes(0), load_codes(1)]
         nc.sync.dma_start(out=window[:], in_=mem)
         nc.sync.dma_start(offsets[:], slot)
-        load_scales(nc.sync, slice(T // 2, T), range(1, 4))
+        load_scales(nc.sync, slice(T // 2, T), range(2, 4))
         x_codes.append(load_codes(2))
         x_codes.append(load_codes(3))
+        spare = keep.tile([P, U], F32, name="spare", align_bytes=64)
+        nc.sync.dma_start(out=spare[:], in_=mem)
 
         def by_slot(c0, width):
             return window[:].indirect(offsets[:, c0 // 16 : (c0 + width) // 16])
@@ -112,9 +113,10 @@ def tile_picked_wgmem_tanh_l_kernel(tc, x_words, x_scales, mem, w1, w2, slot, ou
             for z in range(PASSES):
                 quantise(name, z)
 
-        stay = keep.tile([P, T], F32, name="stay", align_bytes=64)
+        early = keep.tile([P, 128 + T], F32, name="early", align_bytes=64)
+        stay = early[:, 128 : 128 + T]
         minus_cand = keep.tile([P, T], F32, name="minus_cand", align_bytes=64)
-        old = keep.tile([P, 448], F32, name="old", align_bytes=64)
+        old = keep.tile([P, 256], F32, name="old", align_bytes=64)
         kept = keep.tile([P, T], F32, name="kept", align_bytes=64)
         fresh = keep.tile([P, T], F32, name="fresh", align_bytes=64)
         new_b = keep.tile([P, 256], F32, name="new_b", align_bytes=64)
@@ -127,9 +129,10 @@ def tile_picked_wgmem_tanh_l_kernel(tc, x_words, x_scales, mem, w1, w2, slot, ou
             acc = product("gate", c0, 256, "gate%d" % c0)
             nc.scalar.activation(stay[:, c0 : c0 + 256], acc[:], ACT.Sigmoid, scale=-1.0)
 
-        def blend(c0, width, dst=fresh):
+        def blend(c0, width, dst=fresh, d0=None):
+            d0 = c0 if d0 is None else d0
             cols = slice(c0, c0 + width)
-            nc.vector.scalar_tensor_tensor(dst[:, cols], stay[:, cols], 1.0, minus_cand[:, cols], ALU.subtract, ALU.mult)
+            nc.vector.scalar_tensor_tensor(dst[:, d0 : d0 + width], stay[:, cols], 1.0, minus_cand[:, cols], ALU.subtract, ALU.mult)
 
         def gather(c0, width):
             cols = slice(c0, c0 + width)
@@ -143,19 +146,20 @@ def tile_picked_wgmem_tanh_l_kernel(tc, x_words, x_scales, mem, w1, w2, slot, ou
             gates(c0)
             candidates(c0)
         blend(0, 256)
-        gather(256, 256)
-        gather(0, 256)
-        blend(256, 256, stay)
-        nc.scalar.activation(old[:], by_slot(512, 448), ACT.Copy)
+        gather(0, 128)
+        gather(128, 128)
+        nc.vector.scalar_tensor_tensor(early[:, 0:256], stay[:, 256:512], 1.0, minus_cand[:, 256:512], ALU.subtract, ALU.mult)
+        nc.scalar.activation(old[:], by_slot(256, 256), ACT.Copy)
+        nc.vector.tensor_tensor(kept[:, 256:512], old[:], stay[:, 256:512], ALU.mult)
         scatter(0, 256)
-        nc.vector.tensor_tensor(new_b[:], kept[:, 256:512], stay[:, 256:512], ALU.add)
+        nc.vector.tensor_tensor(new_b[:], kept[:, 256:512], early[:, 0:256], ALU.add)
         for c0 in (512, 768):
             candidates(c0)
             gates(c0)
         gather(960, 64)
         nc.scalar.activation(by_slot(256, 256), new_b[:], ACT.Copy)
-        nc.vector.tensor_tensor(kept[:, 512:960], old[:], stay[:, 512:960], ALU.mult)
         blend(512, 512)
+        nc.vector.tensor_tensor(kept[:, 512:960], spare[:].indirect(offsets[:, 32:60]), stay[:, 512:960], ALU.mult)
         scatter(512, 512)
 
         nc.sync.dma_start(out=out, in_=window[:])

@@ -29,12 +29,13 @@ def tile_picked_wgmem_tanh_l_kernel(tc, x_words, x_scales, mem, w1, w2, slot, ou
 
         offsets = keep.tile([P, T // 16], U16, name="offsets")
         window = keep.tile([P, U], F32, name="window", align_bytes=64)
-        x_plane = keep.tile([P, PASSES, T], U8, name="x_plane", align_bytes=64)
+        x_plane = [keep.tile([P, PASSES, T // 2], U8, name="x_plane%d" % h, align_bytes=64) for h in range(2)]
 
-        def load_scales(queue, cols, quadrants):
+        def load_scales(queue, h, quadrants):
+            cols = slice(h * T // 2, (h + 1) * T // 2)
             for q in quadrants:
                 queue.dma_start(
-                    out=x_plane[32 * q : 32 * q + 4, :, cols].bitcast(I32),
+                    out=x_plane[h][32 * q + 4 * h : 32 * q + 4 * h + 4].bitcast(I32),
                     in_=x_scales[:, 4 * q : 4 * q + 4, cols].rearrange("z r c -> r z c").bitcast(I32),
                 )
 
@@ -46,22 +47,24 @@ def tile_picked_wgmem_tanh_l_kernel(tc, x_words, x_scales, mem, w1, w2, slot, ou
             nc.sync.dma_start(out=codes[:].bitcast(I32), in_=words[:, :, c0 : c0 + width])
             return codes
 
-        load_scales(nc.scalar, slice(0, T), range(2))
+        load_scales(nc.scalar, 0, range(4))
         raw = {}
 
-        def load_weight(name, w):
-            both = keep.tile([P, PASSES, PACK, N], F32, name="raw_" + name, align_bytes=64)
-            nc.sync.dma_start(out=both[:], in_=w.rearrange("(z p j) m -> p z j m", z=PASSES, j=PACK))
-            for z in range(PASSES):
-                raw[name, z] = both[:, z]
+        def load_weight(name, w, loads):
+            rows = w.rearrange("(z p j) m -> p z j m", z=PASSES, j=PACK)
+            each = PASSES // loads
+            for z0 in range(0, PASSES, each):
+                part = keep.tile([P, each, PACK, N], F32, name="raw_%s%d" % (name, z0), align_bytes=64)
+                nc.sync.dma_start(out=part[:], in_=rows[:, z0 : z0 + each])
+                for i in range(each):
+                    raw[name, z0 + i] = part[:, i]
 
-        load_weight("gate", w2)
-        load_scales(nc.sync, slice(0, T // 2), range(2, 4))
-        load_weight("cand", w1)
+        load_weight("gate", w2, 2)
+        load_weight("cand", w1, 1)
         x_codes = [load_codes(0), load_codes(1)]
         nc.sync.dma_start(out=window[:], in_=mem)
         nc.sync.dma_start(offsets[:], slot)
-        load_scales(nc.sync, slice(T // 2, T), range(2, 4))
+        load_scales(nc.sync, 1, range(4))
         x_codes.append(load_codes(2))
         x_codes.append(load_codes(3))
         spare = keep.tile([P, U], F32, name="spare", align_bytes=64)
@@ -73,7 +76,7 @@ def tile_picked_wgmem_tanh_l_kernel(tc, x_words, x_scales, mem, w1, w2, slot, ou
         def x_operands(z, c0, width):
             c = [i for i, (l0, lw) in enumerate(LOADS) if l0 <= c0 < l0 + lw][0]
             l0 = LOADS[c][0]
-            return x_codes[c][:, z, c0 - l0 : c0 - l0 + width].bitcast(FP8X4), x_plane[:, z, c0 : c0 + width]
+            return x_codes[c][:, z, c0 - l0 : c0 - l0 + width].bitcast(FP8X4), x_plane[c0 // 512][4 * (c0 // 512) : P, z, c0 % 512 : c0 % 512 + width]
 
         w_codes, w_plane, grouped = {}, {}, {}
 
@@ -119,7 +122,6 @@ def tile_picked_wgmem_tanh_l_kernel(tc, x_words, x_scales, mem, w1, w2, slot, ou
         old = keep.tile([P, 256], F32, name="old", align_bytes=64)
         kept = keep.tile([P, T], F32, name="kept", align_bytes=64)
         fresh = keep.tile([P, T], F32, name="fresh", align_bytes=64)
-        new_b = keep.tile([P, 256], F32, name="new_b", align_bytes=64)
 
         def candidates(c0):
             acc = product("cand", c0, 256, "cand%d" % c0)
@@ -152,14 +154,14 @@ def tile_picked_wgmem_tanh_l_kernel(tc, x_words, x_scales, mem, w1, w2, slot, ou
         nc.scalar.activation(old[:], by_slot(256, 256), ACT.Copy)
         nc.vector.tensor_tensor(kept[:, 256:512], old[:], stay[:, 256:512], ALU.mult)
         scatter(0, 256)
-        nc.vector.tensor_tensor(new_b[:], kept[:, 256:512], early[:, 0:256], ALU.add)
         for c0 in (512, 768):
-            candidates(c0)
             gates(c0)
-        gather(960, 64)
+            candidates(c0)
+        new_b = keep.tile([P, 256], F32, name="new_b", tag="x_codes3", align_bytes=64)
+        nc.vector.tensor_tensor(new_b[:], kept[:, 256:512], early[:, 0:256], ALU.add)
         nc.scalar.activation(by_slot(256, 256), new_b[:], ACT.Copy)
         blend(512, 512)
-        nc.vector.tensor_tensor(kept[:, 512:960], spare[:].indirect(offsets[:, 32:60]), stay[:, 512:960], ALU.mult)
+        nc.vector.tensor_tensor(kept[:, 512:T], spare[:].indirect(offsets[:, 32:64]), stay[:, 512:T], ALU.mult)
         scatter(512, 512)
 
         nc.sync.dma_start(out=out, in_=window[:])

@@ -18,7 +18,10 @@ ALU = mybir.AluOpType
 P = 128
 PACK = 4
 PASSES = K // (P * PACK)
-LOADS = [(0, 256), (256, 256), (512, 256), (768, 256)]
+PIECE = 256
+HALF = T // 2
+SCALAR_GATHERS = 192
+AHEAD = 128
 
 
 def tile_picked_wgmem_tanh_l_kernel(tc, x_words, x_scales, mem, w1, w2, slot, out):
@@ -27,27 +30,32 @@ def tile_picked_wgmem_tanh_l_kernel(tc, x_words, x_scales, mem, w1, w2, slot, ou
         keep = ctx.enter_context(tc.tile_pool(name="keep", bufs=1))
         psum = ctx.enter_context(tc.psum_pool(name="psum", bufs=1))
 
+        first, second, third, fourth = [slice(c0, c0 + PIECE) for c0 in range(0, T, PIECE)]
+        late = slice(HALF, T)
+
+        def halves(cols):
+            middle = (cols.start + cols.stop) // 2
+            return slice(cols.start, middle), slice(middle, cols.stop)
+
         offsets = keep.tile([P, T // 16], U16, name="offsets")
         window = keep.tile([P, U], F32, name="window", align_bytes=64)
-        x_plane = [keep.tile([P, PASSES, T // 2], U8, name="x_plane%d" % h, align_bytes=64) for h in range(2)]
+        spare = keep.tile([P, U], F32, name="spare", align_bytes=64)
+        x_plane = [keep.tile([P, PASSES, HALF], U8, name="x_plane%d" % h, align_bytes=64) for h in range(2)]
 
-        def load_scales(queue, h, quadrants):
-            cols = slice(h * T // 2, (h + 1) * T // 2)
-            for q in quadrants:
+        def load_scales(queue, h):
+            for q in range(4):
                 queue.dma_start(
                     out=x_plane[h][32 * q + 4 * h : 32 * q + 4 * h + 4].bitcast(I32),
-                    in_=x_scales[:, 4 * q : 4 * q + 4, cols].rearrange("z r c -> r z c").bitcast(I32),
+                    in_=x_scales[:, 4 * q : 4 * q + 4, h * HALF : (h + 1) * HALF].rearrange("z r c -> r z c").bitcast(I32),
                 )
 
         words = x_words.rearrange("z p c r -> p z (c r)").bitcast(I32)
+        x_codes = {}
 
-        def load_codes(c):
-            c0, width = LOADS[c]
-            codes = keep.tile([P, PASSES, width], U32, name="x_codes%d" % c, align_bytes=64)
-            nc.sync.dma_start(out=codes[:].bitcast(I32), in_=words[:, :, c0 : c0 + width])
-            return codes
+        def load_codes(cols):
+            x_codes[cols.start] = keep.tile([P, PASSES, PIECE], U32, name="x_codes%d" % cols.start, align_bytes=64)
+            nc.sync.dma_start(out=x_codes[cols.start][:].bitcast(I32), in_=words[:, :, cols])
 
-        load_scales(nc.scalar, 0, range(4))
         raw = {}
 
         def load_weight(name, w, loads):
@@ -59,31 +67,25 @@ def tile_picked_wgmem_tanh_l_kernel(tc, x_words, x_scales, mem, w1, w2, slot, ou
                 for i in range(each):
                     raw[name, z0 + i] = part[:, i]
 
+        load_scales(nc.scalar, 0)
         load_weight("gate", w2, 2)
         load_weight("cand", w1, 1)
-        x_codes = [load_codes(0), load_codes(1)]
+        load_codes(first)
+        load_codes(second)
         nc.sync.dma_start(out=window[:], in_=mem)
         nc.sync.dma_start(offsets[:], slot)
-        load_scales(nc.sync, 1, range(4))
-        x_codes.append(load_codes(2))
-        x_codes.append(load_codes(3))
-        spare = keep.tile([P, U], F32, name="spare", align_bytes=64)
+        load_scales(nc.sync, 1)
+        load_codes(third)
+        load_codes(fourth)
         nc.sync.dma_start(out=spare[:], in_=mem)
 
-        def by_slot(c0, width):
-            return window[:].indirect(offsets[:, c0 // 16 : (c0 + width) // 16])
+        grouped, w_codes, w_plane = {}, {}, {}
 
-        def x_operands(z, c0, width):
-            c = [i for i, (l0, lw) in enumerate(LOADS) if l0 <= c0 < l0 + lw][0]
-            l0 = LOADS[c][0]
-            return x_codes[c][:, z, c0 - l0 : c0 - l0 + width].bitcast(FP8X4), x_plane[c0 // 512][4 * (c0 // 512) : P, z, c0 % 512 : c0 % 512 + width]
-
-        w_codes, w_plane, grouped = {}, {}, {}
-
-        def regroup(copy, name, z, m0, m1):
+        def regroup(copy, name, z):
+            grouped[name, z] = keep.tile([P, N * PACK], BF16, name="grouped_%s%d" % (name, z), align_bytes=64)
             copy(
-                out=grouped[name, z][:, m0 * PACK : m1 * PACK].rearrange("p (c i j) -> p c j i", i=4, j=PACK),
-                in_=raw[name, z][:, :, m0:m1].rearrange("p j (c i) -> p c j i", i=4),
+                out=grouped[name, z][:].rearrange("p (c i j) -> p c j i", i=4, j=PACK),
+                in_=raw[name, z].rearrange("p j (c i) -> p c j i", i=4),
             )
 
         def quantise(name, z):
@@ -91,77 +93,83 @@ def tile_picked_wgmem_tanh_l_kernel(tc, x_words, x_scales, mem, w1, w2, slot, ou
             w_plane[name, z] = keep.tile([P, N], U8, name="plane_%s%d" % (name, z), align_bytes=64)
             nc.vector.quantize_mx(out=w_codes[name, z][:].bitcast(FP8X4), scales=w_plane[name, z][:], in_=grouped[name, z][:])
 
-        for name in ("gate", "cand"):
-            for z in range(PASSES):
-                grouped[name, z] = keep.tile([P, N * PACK], BF16, name="grouped_%s%d" % (name, z), align_bytes=64)
+        banks = []
 
-        def product(name, c0, width, bank):
-            acc = psum.tile([P, width], F32, name="acc_%s%d" % (name, c0), tag=bank)
+        def product(name, cols):
+            acc = psum.tile([P, cols.stop - cols.start], F32, name="acc_%s%d" % (name, cols.start), tag="bank%d" % (len(banks) % 8))
+            banks.append(acc)
+            h, load = cols.start // HALF, cols.start // PIECE * PIECE
             for z in range(PASSES):
-                codes, plane = x_operands(z, c0, width)
                 nc.tensor.matmul_mx(
                     out=acc[:],
                     lhsT=w_codes[name, z][:].bitcast(FP8X4),
                     lhsT_scale=w_plane[name, z][:],
-                    rhs=codes,
-                    rhs_scale=plane,
+                    rhs=x_codes[load][:, z, cols.start - load : cols.stop - load].bitcast(FP8X4),
+                    rhs_scale=x_plane[h][4 * h : P, z, cols.start - h * HALF : cols.stop - h * HALF],
                     start=(z == 0),
                     stop=(z == PASSES - 1),
                 )
             return acc
 
-        for name in ("gate", "cand"):
-            for z in range(PASSES):
-                regroup(nc.vector.tensor_copy, name, z, 0, N)
-            for z in range(PASSES):
-                quantise(name, z)
-
-        early = keep.tile([P, 128 + T], F32, name="early", align_bytes=64)
-        stay = early[:, 128 : 128 + T]
+        early = keep.tile([P, PIECE // 2 + T], F32, name="early", align_bytes=64)
+        stay = early[:, PIECE // 2 : PIECE // 2 + T]
         minus_cand = keep.tile([P, T], F32, name="minus_cand", align_bytes=64)
-        old = keep.tile([P, 256], F32, name="old", align_bytes=64)
         kept = keep.tile([P, T], F32, name="kept", align_bytes=64)
         fresh = keep.tile([P, T], F32, name="fresh", align_bytes=64)
+        old = keep.tile([P, SCALAR_GATHERS], F32, name="old", align_bytes=64)
+        old_late = keep.tile([P, AHEAD], F32, name="old_late", align_bytes=64)
 
-        def candidates(c0):
-            acc = product("cand", c0, 256, "cand%d" % c0)
-            nc.scalar.activation(minus_cand[:, c0 : c0 + 256], acc[:], ACT.Tanh, scale=-1.0)
+        def by_slot(tile, cols):
+            return tile[:].indirect(offsets[:, cols.start // 16 : cols.stop // 16])
 
-        def gates(c0):
-            acc = product("gate", c0, 256, "gate%d" % c0)
-            nc.scalar.activation(stay[:, c0 : c0 + 256], acc[:], ACT.Sigmoid, scale=-1.0)
+        def gates(cols):
+            nc.scalar.activation(stay[:, cols], product("gate", cols)[:], ACT.Sigmoid, scale=-1.0)
 
-        def blend(c0, width, dst=fresh, d0=None):
-            d0 = c0 if d0 is None else d0
-            cols = slice(c0, c0 + width)
-            nc.vector.scalar_tensor_tensor(dst[:, d0 : d0 + width], stay[:, cols], 1.0, minus_cand[:, cols], ALU.subtract, ALU.mult)
+        def candidates(cols):
+            nc.scalar.activation(minus_cand[:, cols], product("cand", cols)[:], ACT.Tanh, scale=-1.0)
 
-        def gather(c0, width):
-            cols = slice(c0, c0 + width)
-            nc.vector.tensor_tensor(kept[:, cols], by_slot(c0, width), stay[:, cols], ALU.mult)
+        def blend(cols, into=None):
+            nc.vector.scalar_tensor_tensor(fresh[:, cols] if into is None else into, stay[:, cols], 1.0, minus_cand[:, cols], ALU.subtract, ALU.mult)
 
-        def scatter(c0, width):
-            cols = slice(c0, c0 + width)
-            nc.vector.tensor_tensor(by_slot(c0, width), kept[:, cols], fresh[:, cols], ALU.add)
+        def gather(tile, cols, shift=0):
+            nc.vector.tensor_tensor(kept[:, cols.start + shift : cols.stop + shift], by_slot(tile, cols), stay[:, cols], ALU.mult)
 
-        for c0 in (0, 256):
-            gates(c0)
-            candidates(c0)
-        blend(0, 256)
-        gather(0, 128)
-        gather(128, 128)
-        nc.vector.scalar_tensor_tensor(early[:, 0:256], stay[:, 256:512], 1.0, minus_cand[:, 256:512], ALU.subtract, ALU.mult)
-        nc.scalar.activation(old[:], by_slot(256, 256), ACT.Copy)
-        nc.vector.tensor_tensor(kept[:, 256:512], old[:], stay[:, 256:512], ALU.mult)
-        scatter(0, 256)
-        for c0 in (512, 768):
-            gates(c0)
-            candidates(c0)
-        new_b = keep.tile([P, 256], F32, name="new_b", tag="x_codes3", align_bytes=64)
-        nc.vector.tensor_tensor(new_b[:], kept[:, 256:512], early[:, 0:256], ALU.add)
-        nc.scalar.activation(by_slot(256, 256), new_b[:], ACT.Copy)
-        blend(512, 512)
-        nc.vector.tensor_tensor(kept[:, 512:T], spare[:].indirect(offsets[:, 32:64]), stay[:, 512:T], ALU.mult)
-        scatter(512, 512)
+        def scatter(cols):
+            nc.vector.tensor_tensor(by_slot(window, cols), kept[:, cols], fresh[:, cols], ALU.add)
+
+        for name in ("gate", "cand"):
+            for z in range(PASSES):
+                regroup(nc.vector.tensor_copy, name, z)
+            for z in range(PASSES):
+                quantise(name, z)
+        gates(first)
+        candidates(first)
+        blend(first)
+        gates(second)
+        for half in halves(second):
+            candidates(half)
+        blend(halves(second)[0], into=early[:, 0 : PIECE // 2])
+
+        by_scalar = slice(PIECE, PIECE + SCALAR_GATHERS)
+        gather(window, first)
+        gather(window, slice(by_scalar.stop, HALF), shift=PIECE)
+        blend(halves(second)[1], into=early[:, PIECE // 2 : PIECE])
+        nc.scalar.activation(old[:], by_slot(window, by_scalar), ACT.Copy)
+        ahead = slice(HALF, HALF + AHEAD)
+        nc.scalar.activation(old_late[:], by_slot(window, ahead), ACT.Copy)
+        nc.vector.tensor_tensor(kept[:, HALF : HALF + SCALAR_GATHERS], old[:], stay[:, by_scalar], ALU.mult)
+        scatter(first)
+
+        for cols in (third, fourth):
+            gates(cols)
+            candidates(cols)
+        new = keep.tile([P, PIECE], F32, name="new", tag="x_codes%d" % fourth.start, align_bytes=64)
+        nc.vector.tensor_tensor(new[:], kept[:, third], early[:, 0:PIECE], ALU.add)
+        nc.scalar.activation(by_slot(window, second), new[:], ACT.Copy)
+
+        blend(late)
+        nc.vector.tensor_tensor(kept[:, ahead], old_late[:], stay[:, ahead], ALU.mult)
+        gather(spare, slice(ahead.stop, T))
+        scatter(late)
 
         nc.sync.dma_start(out=out, in_=window[:])

@@ -43,10 +43,10 @@ def tile_picked_wgmem_tanh_l_kernel(tc, x_words, x_scales, mem, w1, w2, slot, ou
         x_plane = [keep.tile([P, PASSES, HALF], U8, name="x_plane%d" % h, align_bytes=64) for h in range(2)]
 
         def load_scales(queue, h):
-            for q in range(4):
+            for r in range(4):
                 queue.dma_start(
-                    out=x_plane[h][32 * q + 4 * h : 32 * q + 4 * h + 4].bitcast(I32),
-                    in_=x_scales[:, 4 * q : 4 * q + 4, h * HALF : (h + 1) * HALF].rearrange("z r c -> r z c").bitcast(I32),
+                    out=x_plane[h][4 * h + r : P : 32].bitcast(I32),
+                    in_=x_scales[:, r : 16 : 4, h * HALF : (h + 1) * HALF].rearrange("z q c -> q z c").bitcast(I32),
                 )
 
         words = x_words.rearrange("z p c r -> p z (c r)").bitcast(I32)

@@ -21,7 +21,7 @@ PASSES = K // (P * PACK)
 PIECE = 256
 HALF = T // 2
 SCALAR_GATHERS = 192
-AHEAD = 128
+AHEAD = 64
 
 
 def tile_picked_wgmem_tanh_l_kernel(tc, x_words, x_scales, mem, w1, w2, slot, out):
@@ -145,8 +145,8 @@ def tile_picked_wgmem_tanh_l_kernel(tc, x_words, x_scales, mem, w1, w2, slot, ou
         gates(first)
         candidates(first)
         blend(first)
-        gates(second)
         for half in halves(second):
+            gates(half)
             candidates(half)
         blend(halves(second)[0], into=early[:, 0 : PIECE // 2])
 

@@ -21,7 +21,6 @@ PASSES = K // (P * PACK)
 PIECE = 256
 HALF = T // 2
 SCALAR_GATHERS = 192
-AHEAD = 64
 
 
 def tile_picked_wgmem_tanh_l_kernel(tc, x_words, x_scales, mem, w1, w2, slot, out):
@@ -40,14 +39,11 @@ def tile_picked_wgmem_tanh_l_kernel(tc, x_words, x_scales, mem, w1, w2, slot, ou
         offsets = keep.tile([P, T // 16], U16, name="offsets")
         window = keep.tile([P, U], F32, name="window", align_bytes=64)
         spare = keep.tile([P, U], F32, name="spare", align_bytes=64)
-        x_plane = [keep.tile([P, PASSES, HALF], U8, name="x_plane%d" % h, align_bytes=64) for h in range(2)]
+        x_plane = keep.tile([P, PASSES, T], U8, name="x_plane", align_bytes=64)
 
-        def load_scales(queue, h):
-            for r in range(4):
-                queue.dma_start(
-                    out=x_plane[h][4 * h + r : P : 32].bitcast(I32),
-                    in_=x_scales[:, r : 16 : 4, h * HALF : (h + 1) * HALF].rearrange("z q c -> q z c").bitcast(I32),
-                )
+        def load_scales(queue, rows):
+            for r in rows:
+                queue.dma_start(out=x_plane[r:P:32].bitcast(I32), in_=x_scales[:, r:16:4, :].rearrange("z q c -> q z c").bitcast(I32))
 
         words = x_words.rearrange("z p c r -> p z (c r)").bitcast(I32)
         x_codes = {}
@@ -58,23 +54,22 @@ def tile_picked_wgmem_tanh_l_kernel(tc, x_words, x_scales, mem, w1, w2, slot, ou
 
         raw = {}
 
-        def load_weight(name, w, loads):
-            rows = w.rearrange("(z p j) m -> p z j m", z=PASSES, j=PACK)
-            each = PASSES // loads
-            for z0 in range(0, PASSES, each):
-                part = keep.tile([P, each, PACK, N], F32, name="raw_%s%d" % (name, z0), align_bytes=64)
-                nc.sync.dma_start(out=part[:], in_=rows[:, z0 : z0 + each])
-                for i in range(each):
-                    raw[name, z0 + i] = part[:, i]
+        def load_weight(name, w, z0, passes):
+            part = keep.tile([P, passes, PACK, N], F32, name="raw_%s%d" % (name, z0), align_bytes=64)
+            nc.sync.dma_start(out=part[:], in_=w.rearrange("(z p j) m -> p z j m", z=PASSES, j=PACK)[:, z0 : z0 + passes])
+            for i in range(passes):
+                raw[name, z0 + i] = part[:, i]
 
-        load_scales(nc.scalar, 0)
-        load_weight("gate", w2, 2)
-        load_weight("cand", w1, 1)
+        load_scales(nc.scalar, (0, 1))
+        load_weight("gate", w2, 0, 1)
+        load_scales(nc.sync, (2, 3))
+        load_weight("gate", w2, 1, 1)
         load_codes(first)
+        load_weight("cand", w1, 0, 1)
+        load_weight("cand", w1, 1, 1)
         load_codes(second)
         nc.sync.dma_start(out=window[:], in_=mem)
         nc.sync.dma_start(offsets[:], slot)
-        load_scales(nc.sync, 1)
         load_codes(third)
         load_codes(fourth)
         nc.sync.dma_start(out=spare[:], in_=mem)
@@ -98,26 +93,24 @@ def tile_picked_wgmem_tanh_l_kernel(tc, x_words, x_scales, mem, w1, w2, slot, ou
         def product(name, cols):
             acc = psum.tile([P, cols.stop - cols.start], F32, name="acc_%s%d" % (name, cols.start), tag="bank%d" % (len(banks) % 8))
             banks.append(acc)
-            h, load = cols.start // HALF, cols.start // PIECE * PIECE
+            load = cols.start // PIECE * PIECE
             for z in range(PASSES):
                 nc.tensor.matmul_mx(
                     out=acc[:],
                     lhsT=w_codes[name, z][:].bitcast(FP8X4),
                     lhsT_scale=w_plane[name, z][:],
                     rhs=x_codes[load][:, z, cols.start - load : cols.stop - load].bitcast(FP8X4),
-                    rhs_scale=x_plane[h][4 * h : P, z, cols.start - h * HALF : cols.stop - h * HALF],
+                    rhs_scale=x_plane[:, z, cols],
                     start=(z == 0),
                     stop=(z == PASSES - 1),
                 )
             return acc
 
-        early = keep.tile([P, PIECE // 2 + T], F32, name="early", align_bytes=64)
-        stay = early[:, PIECE // 2 : PIECE // 2 + T]
+        stay = keep.tile([P, T], F32, name="stay", align_bytes=64)
         minus_cand = keep.tile([P, T], F32, name="minus_cand", align_bytes=64)
         kept = keep.tile([P, T], F32, name="kept", align_bytes=64)
         fresh = keep.tile([P, T], F32, name="fresh", align_bytes=64)
         old = keep.tile([P, SCALAR_GATHERS], F32, name="old", align_bytes=64)
-        old_late = keep.tile([P, AHEAD], F32, name="old_late", align_bytes=64)
 
         def by_slot(tile, cols):
             return tile[:].indirect(offsets[:, cols.start // 16 : cols.stop // 16])
@@ -128,8 +121,8 @@ def tile_picked_wgmem_tanh_l_kernel(tc, x_words, x_scales, mem, w1, w2, slot, ou
         def candidates(cols):
             nc.scalar.activation(minus_cand[:, cols], product("cand", cols)[:], ACT.Tanh, scale=-1.0)
 
-        def blend(cols, into=None):
-            nc.vector.scalar_tensor_tensor(fresh[:, cols] if into is None else into, stay[:, cols], 1.0, minus_cand[:, cols], ALU.subtract, ALU.mult)
+        def blend(cols):
+            nc.vector.scalar_tensor_tensor(fresh[:, cols], stay[:, cols], 1.0, minus_cand[:, cols], ALU.subtract, ALU.mult)
 
         def gather(tile, cols, shift=0):
             nc.vector.tensor_tensor(kept[:, cols.start + shift : cols.stop + shift], by_slot(tile, cols), stay[:, cols], ALU.mult)
@@ -140,7 +133,6 @@ def tile_picked_wgmem_tanh_l_kernel(tc, x_words, x_scales, mem, w1, w2, slot, ou
         for name in ("gate", "cand"):
             for z in range(PASSES):
                 regroup(nc.vector.tensor_copy, name, z)
-            for z in range(PASSES):
                 quantise(name, z)
         gates(first)
         candidates(first)
@@ -148,15 +140,12 @@ def tile_picked_wgmem_tanh_l_kernel(tc, x_words, x_scales, mem, w1, w2, slot, ou
         for half in halves(second):
             gates(half)
             candidates(half)
-        blend(halves(second)[0], into=early[:, 0 : PIECE // 2])
+            blend(half)
 
         by_scalar = slice(PIECE, PIECE + SCALAR_GATHERS)
         gather(window, first)
         gather(window, slice(by_scalar.stop, HALF), shift=PIECE)
-        blend(halves(second)[1], into=early[:, PIECE // 2 : PIECE])
         nc.scalar.activation(old[:], by_slot(window, by_scalar), ACT.Copy)
-        ahead = slice(HALF, HALF + AHEAD)
-        nc.scalar.activation(old_late[:], by_slot(window, ahead), ACT.Copy)
         nc.vector.tensor_tensor(kept[:, HALF : HALF + SCALAR_GATHERS], old[:], stay[:, by_scalar], ALU.mult)
         scatter(first)
 
@@ -164,12 +153,12 @@ def tile_picked_wgmem_tanh_l_kernel(tc, x_words, x_scales, mem, w1, w2, slot, ou
             gates(cols)
             candidates(cols)
         new = keep.tile([P, PIECE], F32, name="new", tag="x_codes%d" % fourth.start, align_bytes=64)
-        nc.vector.tensor_tensor(new[:], kept[:, third], early[:, 0:PIECE], ALU.add)
+        nc.vector.tensor_tensor(new[:], kept[:, third], fresh[:, second], ALU.add)
         nc.scalar.activation(by_slot(window, second), new[:], ACT.Copy)
 
         blend(late)
-        nc.vector.tensor_tensor(kept[:, ahead], old_late[:], stay[:, ahead], ALU.mult)
-        gather(spare, slice(ahead.stop, T))
+        gather(spare, late)
         scatter(late)
+
 
         nc.sync.dma_start(out=out, in_=window[:])

@@ -31,10 +31,7 @@ def tile_picked_wgmem_tanh_l_kernel(tc, x_words, x_scales, mem, w1, w2, slot, ou
 
         first, second, third, fourth = [slice(c0, c0 + PIECE) for c0 in range(0, T, PIECE)]
         late = slice(HALF, T)
-
-        def halves(cols):
-            middle = (cols.start + cols.stop) // 2
-            return slice(cols.start, middle), slice(middle, cols.stop)
+        halves = slice(PIECE, PIECE + PIECE // 2), slice(PIECE + PIECE // 2, HALF)
 
         offsets = keep.tile([P, T // 16], U16, name="offsets")
         window = keep.tile([P, U], F32, name="window", align_bytes=64)
@@ -46,13 +43,14 @@ def tile_picked_wgmem_tanh_l_kernel(tc, x_words, x_scales, mem, w1, w2, slot, ou
                 queue.dma_start(out=x_plane[r:P:32].bitcast(I32), in_=x_scales[:, r:16:4, :].rearrange("z q c -> q z c").bitcast(I32))
 
         words = x_words.rearrange("z p c r -> p z (c r)").bitcast(I32)
-        x_codes = {}
+        x_codes, raw = {}, {}
 
-        def load_codes(cols):
-            x_codes[cols.start] = keep.tile([P, PASSES, PIECE], U32, name="x_codes%d" % cols.start, align_bytes=64)
-            nc.sync.dma_start(out=x_codes[cols.start][:].bitcast(I32), in_=words[:, :, cols])
-
-        raw = {}
+        def load_codes(z0, passes, cols):
+            part = keep.tile([P, passes, cols.stop - cols.start], U32, name="x_codes%d_%d" % (z0, cols.start), align_bytes=64)
+            nc.sync.dma_start(out=part[:].bitcast(I32), in_=words[:, z0 : z0 + passes, cols])
+            for i in range(passes):
+                for c0 in range(cols.start, cols.stop, PIECE):
+                    x_codes[z0 + i, c0] = part[:, i, c0 - cols.start : c0 - cols.start + PIECE]
 
         def load_weight(name, w, z0, passes):
             part = keep.tile([P, passes, PACK, N], F32, name="raw_%s%d" % (name, z0), align_bytes=64)
@@ -64,21 +62,21 @@ def tile_picked_wgmem_tanh_l_kernel(tc, x_words, x_scales, mem, w1, w2, slot, ou
         load_weight("gate", w2, 0, 1)
         load_scales(nc.sync, (2, 3))
         load_weight("gate", w2, 1, 1)
-        load_codes(first)
         load_weight("cand", w1, 0, 1)
+        load_codes(0, 2, first)
         load_weight("cand", w1, 1, 1)
-        load_codes(second)
+        load_codes(0, 2, second)
         nc.sync.dma_start(out=window[:], in_=mem)
         nc.sync.dma_start(offsets[:], slot)
-        load_codes(third)
-        load_codes(fourth)
+        load_codes(0, 2, third)
+        load_codes(0, 2, fourth)
         nc.sync.dma_start(out=spare[:], in_=mem)
 
         grouped, w_codes, w_plane = {}, {}, {}
 
-        def regroup(copy, name, z):
+        def regroup(name, z):
             grouped[name, z] = keep.tile([P, N * PACK], BF16, name="grouped_%s%d" % (name, z), align_bytes=64)
-            copy(
+            nc.vector.tensor_copy(
                 out=grouped[name, z][:].rearrange("p (c i j) -> p c j i", i=4, j=PACK),
                 in_=raw[name, z].rearrange("p j (c i) -> p c j i", i=4),
             )
@@ -88,23 +86,21 @@ def tile_picked_wgmem_tanh_l_kernel(tc, x_words, x_scales, mem, w1, w2, slot, ou
             w_plane[name, z] = keep.tile([P, N], U8, name="plane_%s%d" % (name, z), align_bytes=64)
             nc.vector.quantize_mx(out=w_codes[name, z][:].bitcast(FP8X4), scales=w_plane[name, z][:], in_=grouped[name, z][:])
 
-        banks = []
+        acc = {}
 
-        def product(name, cols):
-            acc = psum.tile([P, cols.stop - cols.start], F32, name="acc_%s%d" % (name, cols.start), tag="bank%d" % (len(banks) % 8))
-            banks.append(acc)
+        def one_pass(name, cols, z):
+            if z == 0:
+                acc[name, cols.start] = psum.tile([P, cols.stop - cols.start], F32, name="acc_%s%d" % (name, cols.start), tag="bank%d" % (len(acc) % 8))
             load = cols.start // PIECE * PIECE
-            for z in range(PASSES):
-                nc.tensor.matmul_mx(
-                    out=acc[:],
-                    lhsT=w_codes[name, z][:].bitcast(FP8X4),
-                    lhsT_scale=w_plane[name, z][:],
-                    rhs=x_codes[load][:, z, cols.start - load : cols.stop - load].bitcast(FP8X4),
-                    rhs_scale=x_plane[:, z, cols],
-                    start=(z == 0),
-                    stop=(z == PASSES - 1),
-                )
-            return acc
+            nc.tensor.matmul_mx(
+                out=acc[name, cols.start][:],
+                lhsT=w_codes[name, z][:].bitcast(FP8X4),
+                lhsT_scale=w_plane[name, z][:],
+                rhs=x_codes[z, load][:, cols.start - load : cols.stop - load].bitcast(FP8X4),
+                rhs_scale=x_plane[:, z, cols],
+                start=(z == 0),
+                stop=(z == PASSES - 1),
+            )
 
         stay = keep.tile([P, T], F32, name="stay", align_bytes=64)
         minus_cand = keep.tile([P, T], F32, name="minus_cand", align_bytes=64)
@@ -116,10 +112,10 @@ def tile_picked_wgmem_tanh_l_kernel(tc, x_words, x_scales, mem, w1, w2, slot, ou
             return tile[:].indirect(offsets[:, cols.start // 16 : cols.stop // 16])
 
         def gates(cols):
-            nc.scalar.activation(stay[:, cols], product("gate", cols)[:], ACT.Sigmoid, scale=-1.0)
+            nc.scalar.activation(stay[:, cols], acc["gate", cols.start][:], ACT.Sigmoid, scale=-1.0)
 
         def candidates(cols):
-            nc.scalar.activation(minus_cand[:, cols], product("cand", cols)[:], ACT.Tanh, scale=-1.0)
+            nc.scalar.activation(minus_cand[:, cols], acc["cand", cols.start][:], ACT.Tanh, scale=-1.0)
 
         def blend(cols):
             nc.vector.scalar_tensor_tensor(fresh[:, cols], stay[:, cols], 1.0, minus_cand[:, cols], ALU.subtract, ALU.mult)
@@ -132,15 +128,23 @@ def tile_picked_wgmem_tanh_l_kernel(tc, x_words, x_scales, mem, w1, w2, slot, ou
 
         for name in ("gate", "cand"):
             for z in range(PASSES):
-                regroup(nc.vector.tensor_copy, name, z)
+                regroup(name, z)
                 quantise(name, z)
+        for z in range(PASSES):
+            one_pass("gate", first, z)
         gates(first)
+        one_pass("cand", first, 0)
+        for z in range(PASSES):
+            one_pass("gate", second, z)
+        gates(second)
+        one_pass("cand", first, 1)
         candidates(first)
         blend(first)
-        for half in halves(second):
-            gates(half)
-            candidates(half)
-            blend(half)
+        for cols in halves:
+            for z in range(PASSES):
+                one_pass("cand", cols, z)
+            candidates(cols)
+            blend(cols)
 
         by_scalar = slice(PIECE, PIECE + SCALAR_GATHERS)
         gather(window, first)
@@ -150,15 +154,16 @@ def tile_picked_wgmem_tanh_l_kernel(tc, x_words, x_scales, mem, w1, w2, slot, ou
         scatter(first)
 
         for cols in (third, fourth):
-            gates(cols)
-            candidates(cols)
-        new = keep.tile([P, PIECE], F32, name="new", tag="x_codes%d" % fourth.start, align_bytes=64)
+            for name, activate in (("gate", gates), ("cand", candidates)):
+                for z in range(PASSES):
+                    one_pass(name, cols, z)
+                activate(cols)
+        new = keep.tile([P, PIECE], F32, name="new", tag="x_codes0_768", align_bytes=64)
         nc.vector.tensor_tensor(new[:], kept[:, third], fresh[:, second], ALU.add)
         nc.scalar.activation(by_slot(window, second), new[:], ACT.Copy)
 
         blend(late)
         gather(spare, late)
         scatter(late)
-
 
         nc.sync.dma_start(out=out, in_=window[:])

from contextlib import ExitStack

import concourse.mybir as mybir

K, T, N, U = 1024, 1024, 128, 2048
FLOPS = 2 * 2 * K * T * N

F32 = mybir.dt.float32
BF16 = mybir.dt.bfloat16
I32 = mybir.dt.int32
U32 = mybir.dt.uint32
U16 = mybir.dt.uint16
U8 = mybir.dt.uint8
FP8X4 = mybir.dt.float8_e4m3fn_x4
ACT = mybir.ActivationFunctionType
ALU = mybir.AluOpType

P = 128
PACK = 4
PASSES = K // (P * PACK)
PIECE = 256
HALF = T // 2
SCALAR_GATHERS = 192


def tile_picked_wgmem_tanh_l_kernel(tc, x_words, x_scales, mem, w1, w2, slot, out):
    nc = tc.nc
    with ExitStack() as ctx:
        keep = ctx.enter_context(tc.tile_pool(name="keep", bufs=1))
        psum = ctx.enter_context(tc.psum_pool(name="psum", bufs=1))

        first, second, third, fourth = [slice(c0, c0 + PIECE) for c0 in range(0, T, PIECE)]
        late = slice(HALF, T)
        halves = slice(PIECE, PIECE + PIECE // 2), slice(PIECE + PIECE // 2, HALF)

        offsets = keep.tile([P, T // 16], U16, name="offsets")
        window = keep.tile([P, U], F32, name="window", align_bytes=64)
        spare = keep.tile([P, U], F32, name="spare", align_bytes=64)
        x_plane = keep.tile([P, PASSES, T], U8, name="x_plane", align_bytes=64)

        def load_scales(queue, rows):
            for r in rows:
                queue.dma_start(out=x_plane[r:P:32].bitcast(I32), in_=x_scales[:, r:16:4, :].rearrange("z q c -> q z c").bitcast(I32))

        words = x_words.rearrange("z p c r -> p z (c r)").bitcast(I32)
        x_codes, raw = {}, {}

        def load_codes(z0, passes, cols):
            part = keep.tile([P, passes, cols.stop - cols.start], U32, name="x_codes%d_%d" % (z0, cols.start), align_bytes=64)
            nc.sync.dma_start(out=part[:].bitcast(I32), in_=words[:, z0 : z0 + passes, cols])
            for i in range(passes):
                for c0 in range(cols.start, cols.stop, PIECE):
                    x_codes[z0 + i, c0] = part[:, i, c0 - cols.start : c0 - cols.start + PIECE]

        def load_weight(name, w, z0, passes):
            part = keep.tile([P, passes, PACK, N], F32, name="raw_%s%d" % (name, z0), align_bytes=64)
            nc.sync.dma_start(out=part[:], in_=w.rearrange("(z p j) m -> p z j m", z=PASSES, j=PACK)[:, z0 : z0 + passes])
            for i in range(passes):
                raw[name, z0 + i] = part[:, i]

        load_scales(nc.scalar, (0, 1))
        load_weight("gate", w2, 0, 1)
        load_scales(nc.sync, (2, 3))
        load_weight("gate", w2, 1, 1)
        load_weight("cand", w1, 0, 1)
        load_codes(0, 2, first)
        load_weight("cand", w1, 1, 1)
        load_codes(0, 2, second)
        nc.sync.dma_start(out=window[:], in_=mem)
        nc.sync.dma_start(offsets[:], slot)
        load_codes(0, 2, third)
        load_codes(0, 2, fourth)
        nc.sync.dma_start(out=spare[:], in_=mem)

        grouped, w_codes, w_plane = {}, {}, {}

        def regroup(name, z):
            grouped[name, z] = keep.tile([P, N * PACK], BF16, name="grouped_%s%d" % (name, z), align_bytes=64)
            nc.vector.tensor_copy(
                out=grouped[name, z][:].rearrange("p (c i j) -> p c j i", i=4, j=PACK),
                in_=raw[name, z].rearrange("p j (c i) -> p c j i", i=4),
            )

        def quantise(name, z):
            w_codes[name, z] = keep.tile([P, N], U32, name="codes_%s%d" % (name, z), align_bytes=64)
            w_plane[name, z] = keep.tile([P, N], U8, name="plane_%s%d" % (name, z), align_bytes=64)
            nc.vector.quantize_mx(out=w_codes[name, z][:].bitcast(FP8X4), scales=w_plane[name, z][:], in_=grouped[name, z][:])

        acc = {}

        def one_pass(name, cols, z):
            if z == 0:
                acc[name, cols.start] = psum.tile([P, cols.stop - cols.start], F32, name="acc_%s%d" % (name, cols.start), tag="bank%d" % (len(acc) % 8))
            load = cols.start // PIECE * PIECE
            nc.tensor.matmul_mx(
                out=acc[name, cols.start][:],
                lhsT=w_codes[name, z][:].bitcast(FP8X4),
                lhsT_scale=w_plane[name, z][:],
                rhs=x_codes[z, load][:, cols.start - load : cols.stop - load].bitcast(FP8X4),
                rhs_scale=x_plane[:, z, cols],
                start=(z == 0),
                stop=(z == PASSES - 1),
            )

        stay = keep.tile([P, T], F32, name="stay", align_bytes=64)
        minus_cand = keep.tile([P, T], F32, name="minus_cand", align_bytes=64)
        kept = keep.tile([P, T], F32, name="kept", align_bytes=64)
        fresh = keep.tile([P, T], F32, name="fresh", align_bytes=64)
        old = keep.tile([P, SCALAR_GATHERS], F32, name="old", align_bytes=64)

        def by_slot(tile, cols):
            return tile[:].indirect(offsets[:, cols.start // 16 : cols.stop // 16])

        def gates(cols):
            nc.scalar.activation(stay[:, cols], acc["gate", cols.start][:], ACT.Sigmoid, scale=-1.0)

        def candidates(cols):
            nc.scalar.activation(minus_cand[:, cols], acc["cand", cols.start][:], ACT.Tanh, scale=-1.0)

        def blend(cols):
            nc.vector.scalar_tensor_tensor(fresh[:, cols], stay[:, cols], 1.0, minus_cand[:, cols], ALU.subtract, ALU.mult)

        def gather(tile, cols, shift=0):
            nc.vector.tensor_tensor(kept[:, cols.start + shift : cols.stop + shift], by_slot(tile, cols), stay[:, cols], ALU.mult)

        def scatter(cols):
            nc.vector.tensor_tensor(by_slot(window, cols), kept[:, cols], fresh[:, cols], ALU.add)

        for name in ("gate", "cand"):
            for z in range(PASSES):
                regroup(name, z)
                quantise(name, z)
        for z in range(PASSES):
            one_pass("gate", first, z)
        gates(first)
        one_pass("cand", first, 0)
        for z in range(PASSES):
            one_pass("gate", second, z)
        gates(second)
        one_pass("cand", first, 1)
        candidates(first)
        blend(first)
        for cols in halves:
            for z in range(PASSES):
                one_pass("cand", cols, z)
            candidates(cols)
            blend(cols)

        by_scalar = slice(PIECE, PIECE + SCALAR_GATHERS)
        gather(window, first)
        gather(window, slice(by_scalar.stop, HALF), shift=PIECE)
        nc.scalar.activation(old[:], by_slot(window, by_scalar), ACT.Copy)
        nc.vector.tensor_tensor(kept[:, HALF : HALF + SCALAR_GATHERS], old[:], stay[:, by_scalar], ALU.mult)
        scatter(first)

        for cols in (third, fourth):
            for name, activate in (("gate", gates), ("cand", candidates)):
                for z in range(PASSES):
                    one_pass(name, cols, z)
                activate(cols)
        new = keep.tile([P, PIECE], F32, name="new", tag="x_codes0_768", align_bytes=64)
        nc.vector.tensor_tensor(new[:], kept[:, third], fresh[:, second], ALU.add)
        nc.scalar.activation(by_slot(window, second), new[:], ACT.Copy)

        blend(late)
        gather(spare, late)
        scatter(late)

        nc.sync.dma_start(out=out, in_=window[:])
